import numpy as np, ml_dtypes
CORES = [35,38,43,46]
N = 4
BF = ml_dtypes.bfloat16
W, S, P, M, RO = 4096, 256, 16, 4, 6
DIST = (1, 2, 3)
ST = 16 // M
def rho(d, h):
    return (((d * (2 * h + 1)) >> 1) + 613 * h) & (W - 1)
def lay(a):
    n = a.shape[-1]; return np.ascontiguousarray(a.reshape(N, 8, S // 16, 16, n).transpose(0, 1, 3, 2, 4)).reshape(N, 128, -1)
def unlay(a, n):
    return np.ascontiguousarray(a.astype(np.int64).reshape(N, 8, 16, S // 16, n).transpose(0, 1, 3, 2, 4)).reshape(N, 8, S, n)
def records(x):
    return np.ascontiguousarray(x.astype(np.int16).transpose(0, 1, 3, 2)).reshape(N * 8 * W, 16)
def heard(rec, d, h):
    return rec[np.arange(N * 8).reshape(N, 8, 1, 1) * W + rho(d, h)]
def apart(u, v):
    return np.add.reduce(np.abs(u - v), axis=-1, dtype=np.int64)
def pack(x, d, h, th, a):
    return {"X": np.ascontiguousarray(x.reshape(N, 128, W)).astype(np.float32).astype(BF), "D": lay(d).astype(np.int32), "H": lay(h).astype(np.int32),
            "th": lay(th[..., None]).astype(np.int32), "A": lay(a[..., None]).astype(np.int32)}
def runs(rng, stay):
    new = rng.random((N, 8, S, P)) >= stay; new[..., 0] = True
    i = np.maximum.accumulate(np.where(new, np.arange(P), 0), axis=-1)
    return np.take_along_axis(rng.integers(0, 16, (N, 8, S, P)), i, -1)
def setup_inputs(rng):
    x = rng.integers(-128, 128, (N, 8, 16, W)); d = rng.integers(0, W, (N, 8, S, P))
    h = runs(rng, rng.choice(np.array([0.3, 0.6, 0.8, 0.95]), (N, 8, S, 1)))
    return pack(x, d, h, rng.integers(1000, 1900, (N, 8, S)), rng.integers(0, 64, (N, 8, S)))
def setup_inputs_spread(rng):
    x = np.floor(rng.integers(-128, 128, (N, 8, 16, W)) * np.exp2(-rng.integers(0, 7, (N, 8, 1, W)).astype(np.float64))).astype(np.int64)
    d = np.floor(W * rng.random((N, 8, S, P)) ** rng.integers(1, 5, (N, 8, S, 1))).astype(np.int64); d = np.minimum(d, W - 1)
    h = runs(rng, rng.random((N, 8, S, 1)))
    th = np.minimum(np.floor(np.exp2(12 * np.sqrt(rng.random((N, 8, S))))).astype(np.int64) - 1, 4079)
    return pack(x, d, h, th, rng.integers(0, 64, (N, 8, S)))
def setup_inputs_ends(rng):
    kind = rng.integers(0, 10, (N, 8, 1, W)); top = np.where(kind < 3, 0, np.where(kind < 6, 1, rng.integers(0, 2, (N, 8, 16, W))))
    x = np.where(top == 1, 127, -128); x = x + np.where((kind == 9) & (rng.random((N, 8, 16, W)) < 0.5), 1 - 2 * top, 0)
    end = (W - 1) * rng.integers(0, 2, (N, 8, S, P))
    d = np.where(rng.random((N, 8, S, P)) < 0.8, end, rng.integers(0, W, (N, 8, S, P)))
    h = 15 * (runs(rng, 0.8) & 1); th = 4079 * rng.integers(0, 2, (N, 8, S)); a = 63 * rng.integers(0, 2, (N, 8, S))
    six = np.arange(16); c0 = rho(0, six); c1 = rho(W - 1, six); both = np.concatenate([c0, c1])
    last = int(np.argmax(rho(np.arange(W), 15) == W - 1)); d[:, :, S - 2, P - 1] = last; h[:, :, S - 2, P - 1] = 15
    chain = [0, W - 1, 0]
    for j in range(RO): chain.append((13 * chain[-1] + 4080) & (W - 1))
    far = rho(np.array(chain)[:, None], six[None, :]).reshape(-1)
    x[N - 1, 7][:, far] = 127; x[N - 1, 7][:, W - 1] = 127
    x[N - 2, 7][:, both] = -128
    for m in (1, 2, M - 1): x[N - 2, 7][:, [c0[ST * m], c1[ST * m]]] = 127
    for l in (0, S - 1):
        for q in [(N - 1 + j) % N for j in DIST]:
            x[q, 7][:, [c0[15], c1[15]]] = -128; d[q, 7, l] = end[q, 7, l]; h[q, 7, l] = 15; th[q, 7, l] = 4079; a[q, 7, l] = 63
        d[N - 1, 7, l] = end[N - 1, 7, l]; d[N - 1, 7, l, 0] = 0; h[N - 1, 7, l] = 15; th[N - 1, 7, l] = 0; a[N - 1, 7, l] = 63
    for l in (1, S - 3):
        for q in (N - 2, N - 1): d[q, 7, l] = end[q, 7, l]; h[q, 7, l] = 15; th[q, 7, l] = 4079; a[q, 7, l] = 0
    x[0, 7][:, W - 1] = -128; x[0, 7][:, 0] = 127
    for q in (0, N - 1): d[q, 7, S - 2, :P - 1] = 0; h[q, 7, S - 2, :P - 1] = 0; th[q, 7, S - 2] = 4079; a[q, 7, S - 2] = 0
    x[N - 1, 6][:, both] = 127; x[0, 6][:, both] = -128; x[N - 1, 6, 15, c1[ST]] = 126
    for l in (0, S - 1):
        for q in (0, N - 1): d[q, 6, l] = 0; d[q, 6, l, P - 1] = W - 1; h[q, 6, l] = 15; th[q, 6, l] = 4079; a[q, 6, l] = 0
    return pack(x, d, h, th, a)
def setup_inputs_corners(rng):
    k = np.arange(P); x = rng.integers(-128, 128, (N, 8, 16, W)); x[..., 0::2] = rng.integers(-4, 5, (N, 8, 16, W // 2))
    u = rng.integers(0, 16, (N, 8, S, 1)); v = rng.integers(0, 16, (N, 8, S, 1)); c = rng.integers(0, P, (N, 8, S, 1)); e = c + rng.integers(1, P, (N, 8, S, 1)); full = np.zeros((N, 8, S, P), np.int64)
    h = np.choose(rng.integers(0, 6, (N, 8, S, 1)) + full, [u + full, np.where(k % 2 == 0, u, v) + full, (u + k) & 15, np.where(k < c, u, v) + full, np.where((k >= c) & (k < e), v, u) + full, runs(rng, 0.7)])
    first = rng.choice(np.array([0, 0, 1, P // 2, P // 2 + 1, P - 2, P - 1, P - 1, P]), (1, 8, S, 1)) + np.zeros((N, 1, 1, 1), np.int64)
    loud = np.where(k < first, 0, np.where(k == first, 1, rng.integers(0, 2, (N, 8, S, P))))
    d = rng.integers(0, W, (N, 8, S, P)); d = np.where((rho(d, h) & 1) != loud, d ^ 2, d)
    a = rng.choice(np.array([0, 1, 30, 31, 32, 62, 63]), (N, 8, S))
    s = heard(records(x), d, h); far = apart(s, s[(np.arange(N) + DIST[0]) % N])
    at = np.take_along_axis(far, np.minimum(first, P - 1), -1)[..., 0]
    exact = np.minimum(np.maximum(at - (a & 31) - rng.integers(0, 2, (N, 8, S)), 0), 4079)
    w = rng.random((N, 8, S)); th = np.where(w < 0.45, rng.integers(300, 600, (N, 8, S)), np.where(w < 0.9, exact, np.where(w < 0.95, 0, 4079)))
    return pack(x, d, h, th, a)
def setup_inputs_alike(rng):
    x = np.take_along_axis(rng.integers(0, 2, (N, 8, 16, 7)), np.broadcast_to(rng.integers(0, 7, (N, 8, 1, W)), (N, 8, 16, W)), 3); x[:, 3] = x[0:1, 3]
    d = rng.integers(0, W, (N, 8, S, P)); h = runs(rng, 0.7)
    d[:, 5] = d[:, 5, :, :1]; d[:, :, ::2] = d[0:1, :, ::2]; h[:, :, ::4] = h[0:1, :, ::4]
    return pack(x, d, h, rng.integers(0, 10, (N, 8, S)), rng.choice(np.array([0, 1, 2, 32, 33, 63]), (N, 8, S)))
def setup_inputs_crowds(rng):
    x = rng.integers(-128, 128, (N, 8, 16, W)); d = rng.integers(0, W, (N, 8, S, P)); h = runs(rng, 0.7)
    th = rng.integers(1000, 1900, (N, 8, S)); a = rng.integers(0, 64, (N, 8, S)); o = [int(g) for g in rng.permutation(8)]
    for g in (o[0], o[1], o[4], o[5]): h[:, g] = rng.integers(0, 16, (N, S, 1)); th[:, g] = 0
    for g in (o[3], o[4]):
        x[:, g] = (32 * rng.permutation(8)[:N, None] - 128 + rng.integers(0, 16, (N, 16)))[..., None]; th[:, g] = 0
    still = np.zeros((N, 8, S), bool); still[:, o[2]] = True; still[int(rng.integers(0, 2))::2, o[5]] = True
    still[:, o[6]] = True; still[np.arange(N), o[6], rng.integers(0, S, N)] = False; th[:, o[6]] = 0
    return pack(x, d, h, np.where(still, 4079, th), np.where(still, rng.choice(np.array([1, 31, 63]), (N, 8, S)), a))
def check_inputs(d):
    bad = []
    for k, lo, hi in (("X", -128, 127), ("D", 0, W - 1), ("H", 0, 15), ("th", 0, 4079), ("A", 0, 63)):
        v = np.asarray(d[k]).astype(np.float64)
        if not (np.min(v) >= lo and np.max(v) <= hi): bad.append("range of " + k)
        elif np.any(v != np.floor(v)): bad.append("whole numbers of " + k)
    return bad
def reference(X, D, H, th, A):
    rec = records(X.astype(np.float32).reshape(N, 8, 16, W))
    d = unlay(D, P); h = unlay(H, P); lim = unlay(th, 1); a = unlay(A, 1); k = np.arange(P)
    for rnd in range(RO):
        x = heard(rec, d, h); y = x[(np.arange(N) + DIST[rnd % 3]) % N]; e = apart(x, y)
        over = e > lim + (a & 31); some = np.any(over, axis=-1, keepdims=True); p = np.argmax(over, axis=-1)[..., None]
        hp = np.take_along_axis(h, p, -1); ep = np.take_along_axis(e, p, -1)
        same = h == hp; c = np.add.accumulate(np.where(same, 0, 1), axis=-1)
        run = same & (c == np.take_along_axis(c, p, -1)) & some
        old = np.add.reduce(np.where(run, e, 0), axis=-1, keepdims=True)
        hm = (hp + 1 + ST * np.arange(M) + (ep & (ST - 1))) & 15
        em = np.stack([np.add.reduce(np.where(run, apart(heard(rec, d, hm[..., m:m + 1]), y), 0), axis=-1) for m in range(M)], axis=-1)
        best = np.argmin(em, axis=-1)[..., None]
        better = some & (np.take_along_axis(em, best, -1) < old); mut = some & ~better
        h = np.where(run & better, np.take_along_axis(hm, best, -1), np.where(run & mut & (k >= p), hm[..., :1], h))
        d = np.where(mut & (k == p), (13 * d + e) & (W - 1), d)
        a = a + np.where(mut, 1, 0)
    return {"yD": lay(d).astype(np.float32), "yH": lay(h).astype(np.float32), "yA": lay(a).astype(np.float32)}

from concourse.mybir import AluOpType as OP, AxisListType, ActivationFunctionType as AF

NR = 6
DIST = (1, 2, 3)
S = 256
C = 4
n = S // C
NP = n // 64
m1 = n // NP
PW = 16 * m1
CW = 16 * n
STAB = ((3,),) * C
BIG = float(2 ** 20)
EPS = 1.0 / 64
BIAS = (0.0, 7.0, 14.0, 21.0)
WAKE, NET = 0.1, 5.0

B16, F32, I32, U16 = "bfloat16", "float32", "int32", "uint16"
SCRATCH = {}


def _sb(names, cols, dtype):
    for x in names.split():
        SCRATCH[x] = ("sbuf", [128, cols], dtype)


_sb("Xw", 4096, B16)
_sb("xg yb", NR * S * 16, B16)
_sb("df", S * 16 * 4, B16)
_sb("ae zb", S * 16, B16)
_sb("E dsb d13 lim thq eS k5s ka kb kc fa fb fc rth rA MA MD hsb", S, F32)
_sb("Ac y13 nd sub em hi q m0 ki mh nb am w1 a1 IP IC PG CG pg1 cg1 dfc dfd tD tH p15 c15 inD inH", S, I32)
_sb("Gh K over oh selK sel4 run dqr c0 c1 c2 c3 t1 kp t3 brk", S, B16)
_sb("w4 a4", 4 * S, I32)
_sb("lt", 4 * S, U16)
_sb("lst", S, U16)
_sb("ON ON16 ONB Id IM0 IM1 IM2 IM3 I4 NI LS US L16 DSH R01b R10b gtb x1b nzb y1b", 128, B16)
_sb("WD", 144, B16)
_sb("ONF IF R01 R10", 128, F32)
_sb("inT inA", 16, I32)
_sb("thf Af ya", 16, F32)
NB = 8 // C
for _c in range(C):
    for _x in "abcd"[:NB]:
        SCRATCH["p%s%d" % (_x, _c)] = ("psum", [128, 512], F32)
PLACE = (dict(v="a0", Kp="a1", dq="a2", hs="c0", G0="b0", k0="c0", e="d0", pre="d1", od="d2", d="d3", t2="b0", Gn="b1", Hd="b2", K="b3")
         if NB == 4 else
         dict(v="a0", Kp="a1", dq="a2", hs="a3", G0="a4", k0="b3", e="b0", pre="b1", od="b2", d="b7", t2="a0", Gn="a1", Hd="a2", K="a3"))
LOADS = ["lD", "lH", "lT", "lA", "lX0", "lX1"]
SEMAPHORES = (["qv", "qs", "qt", "qg", "sent"] + LOADS + ["oA"] + ["o%s%d" % (x, c) for x in "DH" for c in range(C)]
              + ["ar%d_%d_%d" % (t, c, p) for t in range(NR) for c in range(C) for p in range(NP)])
WIDE = set(k for k, v in SCRATCH.items() if v[2] != B16 and v[2] != U16)
PS = set(k for k, v in SCRATCH.items() if v[0] == "psum")
CYC = 0.00083 * 1.2


def ap(T, x):
    if len(x) == 4:
        return T[x[0]][:, x[1]:x[2]:x[3]]
    return T[x[0]][:, x[1]:x[2]]


def full(name):
    return (name, 0, SCRATCH[name][1][1])


def sq(name):
    return (name, 0, 128)


def st(x, c):
    return (x, c * n, c * n + n)


def ps(c, x, m=0):
    i = int(PLACE[x][1]) + m
    return ("p%s%d" % (PLACE[x][0], c), i * n, i * n + n)


def build():
    ops = []
    cur = [0.0]

    def add(queue, emit, reads, writes, cost, sem=None, val=1):
        ops.append({"q": queue, "emit": emit, "r": reads, "w": writes, "cost": cost, "pr": cur[0], "sem": sem, "val": val})

    def w_(x):
        return (x[2] - x[1]) // (x[3] if len(x) == 4 else 1)

    def tt(out, a, b, op):
        k = 1 if (a[0] in PS or b[0] in PS) else 2
        add("v", lambda g, T: g.vector.tensor_tensor(out=ap(T, out), in0=ap(T, a), in1=ap(T, b), op=op),
            [a, b], [out], 0.05 + w_(out) * k * CYC)

    def ts(out, a, s1, o0, s2=None, o1=None):
        k = 1 if (out[0] in WIDE or a[0] in WIDE) else 0.5
        if o1 is None:
            f = lambda g, T: g.vector.tensor_scalar(out=ap(T, out), in0=ap(T, a), scalar1=s1, scalar2=None, op0=o0)
        else:
            f = lambda g, T: g.vector.tensor_scalar(out=ap(T, out), in0=ap(T, a), scalar1=s1, scalar2=s2, op0=o0, op1=o1)
        add("v", f, [a], [out], 0.05 + w_(out) * k * CYC)

    def cp(out, a):
        add("v", lambda g, T: g.vector.tensor_copy(out=ap(T, out), in_=ap(T, a)), [a], [out], 0.05 + w_(out) * CYC)

    def vtr(out, a):
        add("v", lambda g, T: g.vector.transpose(out=ap(T, out), in_=ap(T, a)), [a], [out], 0.05 + w_(out) * CYC)

    def gsub(out, off, y):
        add("v", lambda g, T: g.vector.tensor_tensor(out=ap(T, out), in0=T.Xw[:, 0:4096].indirect(ap(T, off)), in1=ap(T, y), op=OP.subtract),
            [off, y, full("Xw")], [out], 0.05 + w_(out) * 1.5 * CYC)

    def act(out, a, func=AF.Identity, bias=0.0, scale=1.0, sc=None):
        add("s", lambda g, T: g.scalar.activation(out=ap(T, out), in_=ap(T, a), func=func, bias=bias, scale=(ap(T, sc) if sc else scale)),
            [a] + ([sc] if sc else []), [out], 0.1 + w_(out) * CYC)

    def sgat(out, off):
        add("s", lambda g, T: g.scalar.activation(out=ap(T, out), in_=T.Xw[:, 0:4096].indirect(ap(T, off)), func=AF.Copy),
            [off, full("Xw")], [out], 0.065 + w_(out) * 1.5 * CYC)

    def mm(out, pairs):
        cost, r = 0.0, []
        for x in pairs:
            o = x[2] if len(x) > 2 else out
            cost += max(64, w_(o)) * (4 if SCRATCH[x[0][0]][2] == F32 else 1) * 0.00071 * 1.2
            r += [x[0], x[1]]

        def f(g, T):
            i = None
            for j, x in enumerate(pairs):
                o = x[2] if len(x) > 2 else out
                i = g.tensor.matmul(ap(T, o), ap(T, x[0]), ap(T, x[1]), j == 0, j == len(pairs) - 1)
            return i
        add("t", f, r, [out], cost)

    def dma(sem, dst, src, cost, loads):
        add("y", lambda g, T: g.sync.dma_start(out=ap(T, dst), in_=ap(T, src)), [] if loads else [src], [dst] if loads else [], cost, sem, 16)

    cur[0] = 1e5
    dma("lD", full("inD"), ("D", 0, 256), 2.0, True)
    dma("lH", full("inH"), ("H", 0, 256), 2.0, True)
    dma("lX0", ("Xw", 307, 4096), ("X", 0, 3789), 5.0, True)
    dma("lX1", ("Xw", 0, 307), ("X", 3789, 4096), 5.0, True)
    dma("lT", full("inT"), ("th", 0, 16), 2.0, True)
    dma("lA", full("inA"), ("A", 0, 16), 2.0, True)

    def iota(name, pat, cm, w):
        add("g", lambda g, T: g.iota(T[name][:, 0:w], pat, 0, cm), [], [(name, 0, w)], 0.4)
    iota("dfc", [[32, 4], [1016, 2], [1, 16]], -1, 128)
    iota("IP", [[0, 256]], 1, 256)
    iota("cg1", [[0, 8], [1, 2], [0, 16]], 0, 256)
    iota("CG", [[1, 16], [0, 16]], 0, 256)
    iota("dfd", [[1, 128]], -1, 128)
    iota("IC", [[1, 256]], 0, 256)
    iota("c15", [[0, 16], [1, 16]], 0, 256)
    ts(sq("R01"), sq("dfc"), -16.0, OP.is_equal)
    ts(sq("R10"), sq("dfc"), 1016.0, OP.is_equal)
    ts(full("pg1"), full("IP"), 4, OP.arith_shift_right, 1, OP.bitwise_and)
    tt(full("MA"), full("pg1"), full("cg1"), OP.is_equal)
    ts(sq("IF"), sq("dfd"), 0.0, OP.is_equal)
    act(sq("Id"), sq("IF"))
    act(sq("R01b"), sq("R01"))
    act(sq("R10b"), sq("R10"))

    def swap(out, x, a, b, c0, w, eye=("IF", "R01", "R10")):
        tt((a, c0, c0 + w), x, ("MA", c0, c0 + w), OP.mult)
        tt((b, c0, c0 + w), x, (a, c0, c0 + w), OP.subtract)
        o, oc = out[0], out[1]
        mm(out, [(sq(eye[0]), (a, c0, c0 + w)),
                 (sq(eye[1]), (b, c0, c0 + w - 16), (o, oc + 16, oc + w)),
                 (sq(eye[2]), (b, c0 + 16, c0 + w), (o, oc, oc + w - 16))])
    vtr(full("tD"), full("inD"))
    swap(("pa0", 0, 256), full("tD"), "rth", "rA", 0, 256)
    act(full("E"), ("pa0", 0, 256), AF.Identity, 613.0 + EPS)
    vtr(full("tH"), full("inH"))
    swap(("pb0", 0, 256), full("tH"), "over", "oh", 0, 256, ("Id", "R01b", "R10b"))
    act(full("Gh"), ("pb0", 0, 256), AF.Identity, 0.5)

    def ownlist(c, gh):
        tt(st("w1", c), gh, st("E", c), OP.mult)
        ts(st("a1", c), st("w1", c), 4095, OP.bitwise_and)
        cp(st("lst", c), st("a1", c))
    for c in range(C):
        cur[0] = 1e5 - c
        ownlist(c, st("Gh", c))
    cur[0] = 5e4
    ts(full("PG"), full("IP"), 4, OP.arith_shift_right)
    tt(sq("ON"), sq("PG"), sq("CG"), OP.is_equal)
    act(sq("NI"), sq("Id"), scale=-1.0)
    ts(full("p15"), full("PG"), 16.0, OP.mult, 15.0, OP.add)
    tt(("WD", 0, 144), ("IC", 0, 144), ("p15", 0, 144), OP.is_equal)
    ts(sq("gtb"), sq("dfd"), 0.0, OP.is_gt)
    tt(sq("LS"), sq("gtb"), sq("ON"), OP.mult)
    tt(sq("x1b"), sq("LS"), sq("Id"), OP.add)
    act(sq("L16"), sq("x1b"), scale=16.0)
    tt(sq("US"), sq("ON"), sq("x1b"), OP.subtract)
    ts(sq("gtb"), sq("dfd"), 1.0, OP.is_equal)
    tt(sq("gtb"), sq("gtb"), sq("ON"), OP.mult)
    ts(sq("nzb"), sq("c15"), 0.0, OP.is_gt)
    tt(sq("y1b"), sq("Id"), sq("nzb"), OP.mult)
    tt(sq("DSH"), sq("y1b"), sq("gtb"), OP.subtract)
    act(sq("ON16"), sq("ON"), scale=16.0)
    act(sq("ONF"), sq("ON"), scale=16.0)
    act(sq("ONB"), sq("ON"), scale=-BIG)
    act(sq("I4"), sq("Id"), scale=4.0)
    for m in range(4):
        act(sq("IM%d" % m), sq("Id"), scale=4.0 * m + 0.5)
    add("v", lambda g, T: g.vector.memset(T["c3"][:, 0:256], 0.75), [], [full("c3")], 0.2)
    ts(full("p15"), full("IP"), 15, OP.bitwise_and)
    tt(full("MD"), full("p15"), full("c15"), OP.is_equal)
    cp(full("thf"), full("inT"))
    cp(full("Af"), full("inA"))
    for b in range(16):
        act(("rth", 16 * b, 16 * b + 16), ("MD", 16 * b, 16 * b + 16), AF.Copy, sc=("thf", b, b + 1))
    for b in range(16):
        act(("rA", 16 * b, 16 * b + 16), ("MD", 16 * b, 16 * b + 16), AF.Copy, sc=("Af", b, b + 1))
    mm(("pa1", 0, 256), [(sq("ONF"), full("rth"))])
    mm(("pb1", 0, 256), [(sq("ONF"), full("rA"))])
    act(full("thq"), ("pa1", 0, 256), scale=1.0 / 16)
    ts(full("Ac"), ("pb1", 0, 256), 1.0 / 16, OP.mult)

    def limit(c):
        ts(st("am", c), st("Ac", c), 31, OP.bitwise_and)
        tt(st("lim", c), st("am", c), st("thq", c), OP.add)

    def signs(c):
        act(ps(c, "d"), st("E", c), bias=-613.0 - EPS)
        act(st("d13", c), st("E", c), scale=13.0, bias=-13.0 * (613.0 + EPS))

    def runids(c):
        mm(ps(c, "Hd"), [(sq("DSH"), st("Gh", c))])
        ts(st("brk", c), ps(c, "Hd"), 0.0, OP.not_equal)
        mm(ps(c, "K"), [(sq("L16"), st("brk", c)), (sq("Id"), st("Gh", c))])
        act(st("K", c), ps(c, "K"), bias=0.5)

    def piece(name, c, p, t=0):
        o = t * S * 16 + c * CW + p * PW
        return (name, o, o + PW)

    def dif(c, m, p):
        o = ((c * 4 + m) * NP + p) * PW
        return ("df", o, o + PW)

    def fold16(lhs, src):
        return [(lhs(k), (src[0], src[1] + k, src[2], 16)) for k in range(16)]

    def apart(c, x, y, out):
        for b in range(PW // 512):
            a, o = 512 * b, ("p%s%d" % ("ab"[b % (NB // 2)], c), 0, 512)
            mm(o, [(sq("Id"), (x[0], x[1] + a, x[1] + a + 512)), (sq("NI"), (y[0], y[1] + a, y[1] + a + 512))])
            act((out[0], out[1] + a, out[1] + a + 512), o, AF.Abs)

    def round_(c, t):
        r = lambda x, m=0: ps(c, x, m)
        q = lambda x: st(x, c)
        for p in range(NP):
            src = piece("xg", c, p, t)
            sgat(src, ("lst", c * n + p * m1, c * n + p * m1 + m1))
            add("g", ("send", t, c, p), [src], [], 1.2)
            ops.append({"q": "net", "emit": None, "r": [], "w": [piece("yb", c, p, t)], "cost": NET, "pr": cur[0],
                        "sem": "ar%d_%d_%d" % (t, c, p), "val": 0, "after": len(ops) - 1})
        for p in range(NP):
            apart(c, piece("xg", c, p, t), piece("yb", c, p, t), piece("ae", c, p))
            o = r("e")
            mm((o[0], o[1] + p * m1, o[1] + p * m1 + m1), fold16(lambda k: ("WD", 15 - k, 143 - k), piece("ae", c, p)))
        tt(q("over"), r("e"), q("lim"), OP.is_gt)
        mm(r("v"), [(sq("LS"), q("over"))])
        tt(q("y13"), r("e"), q("d13"), OP.add)
        act(q("eS"), r("e"))
        ts(q("nd"), q("y13"), 4095, OP.bitwise_and)
        tt(q("sub"), q("nd"), r("d"), OP.subtract)
        ts(q("em"), q("sub"), 3, OP.bitwise_and)
        tt(q("oh"), q("over"), r("v"), OP.is_gt)
        tt(q("selK"), q("oh"), q("K"), OP.mult)
        mm(r("Kp"), [(sq("ON"), q("selK"))])
        tt(q("sel4"), q("oh"), q("em"), OP.mult)
        mm(r("hs"), [(sq("ON"), q("selK")), (sq("ON"), q("sel4"))])
        tt(q("run"), q("K"), r("Kp"), OP.is_equal)
        cp(q("hi"), r("hs"))
        ts(q("q"), q("hi"), 3, OP.bitwise_and)
        tt(r("dq"), q("q"), q("Gh"), OP.subtract)
        tt(q("dqr"), q("run"), r("dq"), OP.mult)
        for m in range(4):
            mm(r("G0", m), [(sq("Id"), q("Gh")), (sq("IM%d" % m), q("run")), (sq("Id"), q("dqr"))])
        w4 = lambda x, m: (x, (c * 4 + m) * n, (c * 4 + m + 1) * n)
        all4 = lambda x: (x, c * 4 * n, (c + 1) * 4 * n)
        for m in range(4):
            tt(w4("w4", m), r("G0", m), q("E"), OP.mult)
        ts(all4("a4"), all4("w4"), 4095, OP.bitwise_and)
        cp(all4("lt"), all4("a4"))
        tt(r("od"), q("oh"), q("sub"), OP.mult)
        mm(r("pre"), [(sq("US"), q("oh"))])
        ts(q("m0"), q("hi"), 2, OP.arith_shift_right, 3, OP.bitwise_and)
        for m in range(3):
            ts(q("c%d" % m), q("m0"), float(m), OP.is_gt, m * 0.25, OP.add)
        mm(r("e"), [(sq("ONF"), q("eS"))] + [(sq("Id"), q("c%d" % m)) for m in range(3)] + [(sq("ONB"), q("oh"))])
        act(q("k5s"), r("e"), bias=BIG - 8.75)
        off = lambda m, p: ("lt", (c * 4 + m) * n + p * m1, (c * 4 + m) * n + p * m1 + m1)
        mine = list(STAB[c])
        theirs = [m for m in range(4) if m not in mine]
        for p in range(NP):
            for m in mine:
                sgat(piece("zb", c, p), off(m, p))
                apart(c, piece("zb", c, p), piece("yb", c, p, t), dif(c, m, p))
        for m in theirs:
            for p in range(NP):
                gsub(dif(c, m, p), off(m, p), piece("yb", c, p, t))
                act(dif(c, m, p), dif(c, m, p), AF.Abs)
        for m in mine + theirs:
            for p in range(NP):
                k = r("k0", m)
                mm((k[0], k[1] + p * m1, k[1] + p * m1 + m1),
                   [(sq("I4"), ("c%d" % m, c * n + p * m1, c * n + p * m1 + m1))] + fold16(lambda k: sq("ON16"), dif(c, m, p)))
        tt(q("ka"), r("k0", 3), q("k5s"), OP.min)
        tt(q("kb"), r("k0", 0), q("ka"), OP.min)
        tt(q("kc"), r("k0", 1), q("kb"), OP.min)
        tt(q("ki"), r("k0", 2), q("kc"), OP.min)
        ts(q("mh"), q("ki"), 3, OP.bitwise_and)
        ts(q("nb"), q("ki"), 3, OP.arith_shift_right, 1, OP.bitwise_and)
        tt(q("t1"), q("run"), q("mh"), OP.mult)
        t2 = [(sq("Id"), q("dqr")), (sq("IM0"), q("run")), (sq("I4"), q("t1"))]
        mm(r("t2"), t2)
        tt(q("kp"), r("pre"), q("nb"), OP.mult)
        tt(q("t3"), q("kp"), r("t2"), OP.mult)
        mm(r("Gn"), [(sq("Id"), q("Gh"))] + t2 + [(sq("NI"), q("t3"))])
        tt(r("od"), r("od"), q("nb"), OP.mult)
        tt(q("E"), r("od"), q("E"), OP.add)
        if t < NR - 1:
            ownlist(c, r("Gn"))
            act(q("Gh"), r("Gn"))
            signs(c)
            runids(c)
            tt(q("Ac"), q("Ac"), q("nb"), OP.add)
            limit(c)
        else:
            tt(q("Ac"), q("Ac"), q("nb"), OP.add)
            act(q("hsb"), r("Gn"), bias=-0.5)
            act(q("dsb"), q("E"), bias=-613.0 - EPS)

    def final(c):
        q = lambda x: st(x, c)
        for x, bank, a, b, o, name in (("dsb", "a", "rth", "rA", "fa", "D"), ("hsb", "b", "eS", "k5s", "fb", "H")):
            z = ("p%s%d" % (bank, c), 0, n)
            swap(z, q(x), a, b, c * n, n)
            vtr(q(o), z)
            dma("o%s%d" % (name, c), st("y" + name, c), q(o), 2.0, False)
        tt(q("fc"), q("Ac"), q("MD"), OP.mult)
        for b in range(n // 16):
            a = c * n + 16 * b
            add("v", lambda g, T, a=a: g.vector.tensor_reduce(out=T["ya"][:, a // 16:a // 16 + 1], in_=T["fc"][:, a:a + 16],
                                                              axis=AxisListType.X, op=OP.add),
                [("fc", a, a + 16)], [("ya", a // 16, a // 16 + 1)], 0.1)

    cur[0] = 4e4
    for c in range(C):
        signs(c)
        runids(c)
        limit(c)
    for t in range(NR):
        for c in range(C):
            cur[0] = BIAS[c]
            round_(c, t)
    for c in range(C):
        final(c)
    dma("oA", ("yA", 0, 16), full("ya"), 2.0, False)
    return ops


def schedule(ops):
    hist, bank = {}, {}
    for i, o in enumerate(ops):
        o["dep"], o["ord"] = set(), set()
        if "after" in o:
            o["dep"].add(o["after"])
        for kind, regs in (("r", o["r"]), ("w", o["w"])):
            for x in regs:
                for (j, a2, b2, k2) in hist.get(x[0], ()):
                    if j == i or b2 <= x[1] or x[2] <= a2 or (kind == "r" and k2 == "r"):
                        continue
                    o["dep"].add(j)
        for x in o["r"] + o["w"]:
            if x[0] in PS:
                for j in bank.get(x[0], ()):
                    if j != i:
                        o["ord" if ops[j]["q"] == o["q"] else "dep"].add(j)
        for kind, regs in (("r", o["r"]), ("w", o["w"])):
            for x in regs:
                h = hist.setdefault(x[0], [])
                if kind == "w":
                    h[:] = [y for y in h if not (x[1] <= y[1] and y[2] <= x[2])]
                h.append((i, x[1], x[2], kind))
        for x in o["r"] + o["w"]:
            if x[0] in PS:
                bk = bank.setdefault(x[0], [])
                if bk and ops[bk[-1]]["q"] != o["q"]:
                    bk[:] = []
                if i not in bk:
                    bk.append(i)
    N = len(ops)
    succ = [[] for _ in range(N)]
    need = [0] * N
    for i, o in enumerate(ops):
        o["ord"] -= o["dep"]
        ds = o["dep"] | o["ord"]
        need[i] = len(ds)
        for j in ds:
            succ[j].append(i)
    level = [0.0] * N
    for i in range(N - 1, -1, -1):
        level[i] = ops[i]["cost"] + WAKE + max([level[j] for j in succ[i]], default=0.0)
    ready, order = {}, []
    fin, start, free = [0.0] * N, [0.0] * N, {}
    avail = [i for i in range(N) if need[i] == 0]
    while avail:
        best = None
        for i in avail:
            o = ops[i]
            e = ready.get(i)
            if e is None:
                e = max([fin[j] + WAKE for j in o["dep"]] + [start[j] for j in o["ord"]], default=0.0)
                ready[i] = e
            s = max(e, free.get(o["q"], 0.0)) if o["q"] != "net" else e
            p = o["pr"]
            key = (round(s, 3), -p if p > 1e4 else p - level[i], i)
            if best is None or key < best[0]:
                best = (key, i, s)
        _, i, s = best
        avail.remove(i)
        o = ops[i]
        start[i], fin[i] = s, s + o["cost"]
        free[o["q"]] = s + (o["cost"] if o["q"] != "y" else 0.1)
        order.append(i)
        for j in succ[i]:
            need[j] -= 1
            if need[j] == 0:
                avail.append(j)
    return order, fin


PLAN = {}
SEMOF = {"v": "qv", "s": "qs", "t": "qt", "g": "qg"}


def plan():
    if not PLAN:
        ops = build()
        order, fin = schedule(ops)
        used = set()
        for o in ops:
            used |= o["dep"]
        PLAN["ops"], PLAN["order"], PLAN["used"], PLAN["fin"] = ops, order, used, fin
    return PLAN


def rank_program(g, core, T, topo):
    rank = T.rank_of(core)
    if rank is None:
        return
    P = plan()
    ops, cores = P["ops"], T.cores
    N = len(cores)
    eng = {"v": g.vector, "s": g.scalar, "t": g.tensor, "g": g, "y": g.sync}
    count = {}
    known = {q: {} for q in eng}
    done, sent = {}, 0
    for i in P["order"]:
        o = ops[i]
        q = o["q"]
        if q == "net":
            t = int(o["sem"][2:].split("_")[0])
            v = len(topo.engines(cores[(rank + DIST[t % len(DIST)]) % N], core))
            count[o["sem"]] = v
            done[i] = (o["sem"], v, {})
            continue
        kn = known[q]
        deps = [done[j] for j in sorted(o["dep"]) if j in done]
        want = {}
        for s, v, k in deps:
            if v > kn.get(s, 0):
                want[s] = max(want.get(s, 0), v)
        for s, v, k in deps:
            if kn.get(s, 0) < v:
                for s2, v2 in k.items():
                    if s2 != s and want.get(s2, 0) and want[s2] <= v2:
                        want[s2] = 0
        for s, v in want.items():
            if v:
                eng[q].wait_ge(T.sem[s], v)
        for s, v, k in deps:
            kn[s] = max(kn.get(s, 0), v)
            for s2, v2 in k.items():
                kn[s2] = max(kn.get(s2, 0), v2)
        if isinstance(o["emit"], tuple):
            _, t, c, p = o["emit"]
            dst = cores[(rank - DIST[t % len(DIST)]) % N]
            rid, pid, _s = topo.addr(dst)
            a = t * S * 16 + c * CW + p * PW
            g.remote_dma(out_ap=T["yb"][:, a:a + PW], in_ap=T["xg"][:, a:a + PW], remote_sem=T.sem["ar%d_%d_%d" % (t, c, p)],
                         local_sem=T.sem["sent"], pid=pid, routing_id=rid, dma_engine_mask=topo.mask(core, dst))
            sent += len(topo.engines(core, dst))
            continue
        ins = o["emit"](g, T)
        s = o["sem"] or SEMOF[q]
        if o["sem"] or i in P["used"]:
            ins.then_inc(T.sem[s], o["val"])
            count[s] = count.get(s, 0) + o["val"]
            done[i] = (s, count[s], dict(kn))
    for s, v in count.items():
        g.wait_ge(T.sem[s], v)
    g.wait_ge(T.sem["sent"], sent)
